import numpy as np
import ml_dtypes


def mxq(x, axis, fmt="e4m3"):
    dtype, down = {"e4m3": (ml_dtypes.float8_e4m3fn, 7), "e5m2": (ml_dtypes.float8_e5m2, 14)}[fmt]
    v = np.moveaxis(np.asarray(x, np.float32).astype(ml_dtypes.bfloat16).astype(np.float64), axis, -1)
    blocks = v.reshape(v.shape[:-1] + (-1, 32))
    amax = np.abs(blocks).max(-1, keepdims=True)
    byte = np.maximum(np.where(amax > 0, np.frexp(amax)[1] - 1 + 127, 0) - down, 1)
    scale = np.exp2(byte - 127.0)
    codes = (blocks / scale).astype(np.float32).astype(dtype).astype(np.float64)
    return np.moveaxis((codes * scale).reshape(v.shape), -1, axis)


WIDE = False


def mx_kscale(k):
    if not WIDE:
        return np.ones(k)
    levels = np.array([10, -10, 5, -5, 0])
    if k % 512:
        return np.exp2(np.random.permutation(np.resize(levels, k // 32))).repeat(32)
    a = np.empty((k // 512, 16))
    for p in range(k // 512):
        a[p, :8] = np.random.permutation(np.resize(levels, 8))
        for g in range(8):
            far = levels[np.abs(levels - a[p, g]) >= 10]
            a[p, g + 8] = far[np.random.randint(len(far))]
    return np.exp2(a.ravel()).repeat(32)


def f64(x):
    return np.asarray(x).astype(np.float64)


def striped(idx):
    return np.tile(idx.reshape(-1, 16).T, (8, 1)).astype(np.uint16)


def unstriped(offs):
    return offs[:16].T.reshape(-1).astype(np.int64)


def pack_weight(w):
    k, n = w.shape
    w = f64(np.asarray(w, np.float32).astype(ml_dtypes.bfloat16)).reshape(k // 32, 32, n)
    amax = np.abs(w).max(1)
    byte = np.clip(np.where(amax > 0, np.frexp(amax)[1] - 1 + 127 - 7, 1), 1, 254)
    scaled = (w * np.exp2(127.0 - byte)[:, None, :]).reshape(k, n).astype(np.float32)
    words = np.ascontiguousarray(scaled.reshape(k // 512, 128, 4, n).transpose(0, 1, 3, 2)).astype(ml_dtypes.float8_e4m3fn).view(np.uint8)
    return words, np.ascontiguousarray(byte.astype(np.uint8).reshape(k // 512, 16, n))


def unpack_weight(words, scales):
    g, p, n, _ = words.shape
    vals = np.ascontiguousarray(words).view(ml_dtypes.float8_e4m3fn).astype(np.float64) * np.repeat(np.exp2(scales.astype(np.float64) - 127.0), 8, axis=1)[..., None]
    return vals.transpose(0, 1, 3, 2).reshape(g * 512, n)


K, T, S, N, D = 512, 2048, 512, 256, 3
P = 2 ** 7


def setup_inputs():
    n = np.random.standard_normal
    s = mx_kscale(K)[:, None]
    packed_xT = pack_weight(n((K, T)) * s)
    return {
        "x_words": packed_xT[0],
        "x_scales": packed_xT[1],
        "w1": (n((K, N)) / np.sqrt(K) / s).astype(np.float32),
        "geo": (np.tile(np.random.uniform(0.05, 0.5, (D, 1, S)), (1, P, 1))).astype(np.float32),
        "thr": (np.tile(np.random.uniform(0.5, 0.9, S), (P, 1))).astype(np.float32),
        "rated": (np.tile(np.random.uniform(0.8, 1.6, S), (P, 1))).astype(np.float32),
        "offs": striped(np.random.permutation(T)[:S]),
        "pos1": striped(np.random.permutation(S)[:S]),
        "pos2": striped(np.random.permutation(S)[:S]),
        "pos3": striped(np.random.permutation(S)[:S]),
    }


def reference(x_words, x_scales, w1, geo, thr, rated, offs, pos1, pos2, pos3):
    xq = unpack_weight(x_words, x_scales)[:, unstriped(offs)]
    y = mxq(f64(w1), 0, "e4m3").T @ xq
    free = 0.6 * (np.log(np.exp(y) + 1.0)) + 0.5
    cta = f64(thr)[:1] / (0.5 * free + 0.6)
    ua = free * (-1.0 * (np.sqrt((cta[:, unstriped(pos1)] * f64(geo)[0, :1]) ** 2 + (cta[:, unstriped(pos2)] * f64(geo)[1, :1]) ** 2 + (cta[:, unstriped(pos3)] * f64(geo)[2, :1]) ** 2 + 0.0004)) + 1.0)
    ctb = f64(thr)[:1] / (0.5 * ua + 0.6)
    ub = free * (-1.0 * (np.sqrt((ctb[:, unstriped(pos1)] * f64(geo)[0, :1]) ** 2 + (ctb[:, unstriped(pos2)] * f64(geo)[1, :1]) ** 2 + (ctb[:, unstriped(pos3)] * f64(geo)[2, :1]) ** 2 + 0.0004)) + 1.0)
    return np.minimum(((ub) ** 2) * ub, f64(rated)[:1])

@@ -1,0 +1,202 @@
+import math
+from contextlib import ExitStack
+
+import concourse.mybir as mybir
+from concourse.masks import make_identity
+
+F32 = mybir.dt.float32
+BF16 = mybir.dt.bfloat16
+I32 = mybir.dt.int32
+U32 = mybir.dt.uint32
+U16 = mybir.dt.uint16
+U8 = mybir.dt.uint8
+FP8X4 = mybir.dt.float8_e4m3fn_x4
+ALU = mybir.AluOpType
+ACT = mybir.ActivationFunctionType
+
+K, T, S, N, D = 512, 2048, 512, 256, 3
+P = 128
+PACK = 4
+TILES = N // P
+HALVES = 2
+HALF = S // HALVES
+BLOCKS = HALF // P
+FLOPS = 2 * K * N * S
+
+SHIFT = 5.0 / 6.0
+TINY = 2.0 ** -60
+EPS = 0.0004
+
+
+def tile_picked_ywakef_two_p_kernel(tc, x_words, x_scales, w1, geo, thr, rated, offs, pos1, pos2, pos3, out):
+    nc = tc.nc
+    with ExitStack() as ctx:
+        keep = ctx.enter_context(tc.tile_pool(name="keep", bufs=1))
+        work = ctx.enter_context(tc.tile_pool(name="work", bufs=2))
+        ps_y = ctx.enter_context(tc.psum_pool(name="ps_y", bufs=1))
+        ps_s = ctx.enter_context(tc.psum_pool(name="ps_s", bufs=3))
+        ps_b = ctx.enter_context(tc.psum_pool(name="ps_b", bufs=3))
+
+        offs_sb = keep.tile([P, S // 16], U16, name="offs_sb")
+        pos_sb = [keep.tile([P, S // 16], U16, name="pos_sb%d" % d) for d in range(D)]
+        words = keep.tile([P, T], I32, name="words", align_bytes=64)
+        scales = keep.tile([P, T], U8, name="scales", align_bytes=64)
+        w_raw = keep.tile([P, PACK, N], F32, name="w_raw")
+        geo_sb = keep.tile([P, D, S], F32, name="geo_sb")
+        geo2 = keep.tile([P, D, S], F32, name="geo2")
+        thr_t = keep.tile([P, S // P], F32, name="thr_t")
+        rated_sb = keep.tile([P, S], F32, name="rated_sb")
+        quarter = keep.tile([P, S // P], F32, name="quarter")
+        warm = keep.tile([P, 1], F32, name="warm")
+        ident = keep.tile([P, P], F32, name="ident")
+
+        nc.vector.memset(scales[:].bitcast(I32), 0)
+        nc.gpsimd.memset(quarter[:], 0.25)
+        nc.scalar.activation(warm[:], quarter[:, 0:1], ACT.Sigmoid)
+        make_identity(nc, ident[:])
+
+        nc.sync.dma_start(offs_sb[:], offs)
+        nc.sync.dma_start(w_raw[:], w1.rearrange("(p j) n -> p j n", j=PACK))
+        for q in range(4):
+            nc.sync.dma_start(scales[32 * q : 32 * q + 4, :].bitcast(I32), x_scales[0, 4 * q : 4 * q + 4, :].bitcast(I32))
+        nc.sync.dma_start(words[:], x_words[0].rearrange("p n t -> p (n t)").bitcast(I32))
+        nc.sync.dma_start(geo_sb[:], geo.rearrange("d p s -> p d s"))
+        with nc.allow_non_contiguous_dma(reason="one thrust factor a partition"):
+            nc.sync.dma_start(thr_t[:], thr[0, :].rearrange("(b p) -> p b", p=P))
+        for dst, src in zip(pos_sb, (pos1, pos2, pos3)):
+            nc.sync.dma_start(dst[:], src)
+        nc.sync.dma_start(rated_sb[:], rated)
+
+        w_bf = keep.tile([P, N, PACK], BF16, name="w_bf", align_bytes=64)
+        nc.scalar.activation(w_bf[:], w_raw[:].rearrange("p j n -> p n j"), ACT.Copy, scale=-1.0)
+        xs = keep.tile([P, S], U8, name="xs", align_bytes=64)
+        nc.vector.tensor_copy(xs[:], scales[:].indirect(offs_sb[:]))
+        w_codes = keep.tile([P, N], U32, name="w_codes", align_bytes=64)
+        w_scales = keep.tile([P, N], U8, name="w_scales", align_bytes=64)
+        nc.vector.quantize_mx(out=w_codes[:].bitcast(FP8X4), scales=w_scales[:], in_=w_bf[:].rearrange("p n j -> p (n j)"))
+
+        sig = keep.tile([P, S // P, N], F32, name="sig")
+        neg_y = []
+        for h in range(HALVES):
+            xw = keep.tile([P, HALF], U32, name="xw%d" % h, align_bytes=64)
+            nc.vector.tensor_copy(xw[:], words[:].bitcast(U32).indirect(offs_sb[:, 16 * h : 16 * (h + 1)]))
+            bank = ps_y.tile([P, BLOCKS, N], F32, name="neg_y%d" % h)
+            for b in range(BLOCKS):
+                j0 = h * HALF + b * P
+                nc.tensor.matmul_mx(
+                    out=bank[:, b, :],
+                    lhsT=xw[:, b * P : (b + 1) * P].bitcast(FP8X4),
+                    lhsT_scale=xs[:, j0 : j0 + P],
+                    rhs=w_codes[:].bitcast(FP8X4),
+                    rhs_scale=w_scales[:],
+                    start=True,
+                    stop=True,
+                )
+            nc.scalar.activation(sig[:, h * BLOCKS : (h + 1) * BLOCKS, :], bank[:], ACT.Sigmoid)
+            neg_y.append(bank)
+
+        nc.vector.tensor_tensor(geo2[:], geo_sb[:], geo_sb[:], ALU.mult)
+        thr2 = keep.tile([P, S // P], F32, name="thr2")
+        root_thr = keep.tile([P, S // P], F32, name="root_thr")
+        nc.gpsimd.tensor_tensor(thr2[:], thr_t[:], thr_t[:], ALU.mult)
+        nc.gpsimd.tensor_tensor(root_thr[:], thr2[:], quarter[:], ALU.pow)
+
+        lg = keep.tile([P, S // P, N], F32, name="lg")
+        nc.scalar.activation(lg[:], sig[:], ACT.Ln, bias=TINY, scale=math.e ** (-SHIFT))
+
+        units = [(t, h) for t in range(TILES) for h in range(HALVES)]
+        nsp = {}
+        for t, h in units:
+            nsp[t, h] = keep.tile([P, HALF], F32, name="nsp%d%d" % (t, h))
+            cols = slice(t * P, (t + 1) * P)
+            nc.vector.scalar_tensor_tensor(
+                nsp[t, h][:].rearrange("p (b m) -> p b m", b=BLOCKS), neg_y[h][:, :, cols], SHIFT, lg[:, h * BLOCKS : (h + 1) * BLOCKS, cols], ALU.subtract, ALU.min
+            )
+
+        win = {}
+        for ps in range(2):
+            for t in range(TILES):
+                win[ps, t] = keep.tile([P, S], F32, name="win%d%d" % (ps, t))
+
+        def fresh(name):
+            return keep.tile([P, HALF], F32, name=name)
+
+        def blk(x, b):
+            return x[:, b * P : (b + 1) * P]
+
+        def thrust(ps, t, h, src, scale):
+            a = fresh("th_a%d%d%d" % (ps, t, h))
+            nc.scalar.activation(a[:], src[:], ACT.Abs_reciprocal_sqrt, bias=0.6, scale=scale)
+            ct = work.tile([P, HALF], F32, name="th_ct")
+            back = ps_b.tile([P, HALF], F32, name="back")
+            for b in range(BLOCKS):
+                jb = h * BLOCKS + b
+                nc.scalar.activation(blk(ct, b), blk(a, b), ACT.Square, scale=root_thr[:, jb : jb + 1])
+            for b in range(BLOCKS):
+                nc.tensor.transpose(blk(back, b), blk(ct, b), ident[:])
+            nc.scalar.activation(win[ps, t][:, h * HALF : (h + 1) * HALF], back[:], ACT.Square)
+            return a
+
+        def gathers(ps, t, h, terms):
+            for d in range(D):
+                nc.vector.tensor_tensor(
+                    terms[d][:], win[ps, t][:].indirect(pos_sb[d][:, 16 * h : 16 * (h + 1)]), geo2[:, d, h * HALF : (h + 1) * HALF], ALU.mult
+                )
+            s = ps_s.tile([P, HALF], F32, name="ssum")
+            for b in range(BLOCKS):
+                for d in range(D):
+                    nc.tensor.matmul(blk(s, b), blk(terms[d], b), ident[:], is_transpose=True, start=(d == 0), stop=(d == D - 1))
+            return s
+
+        def root(s, a, r, on_vector):
+            nc.scalar.activation(a[:], s[:], ACT.Abs_reciprocal_sqrt, bias=EPS)
+            if on_vector:
+                nc.vector.scalar_tensor_tensor(r[:], s[:], EPS, a[:], ALU.add, ALU.mult)
+            else:
+                a2 = work.tile([P, HALF], F32, name="wk_a2")
+                nc.scalar.activation(a2[:], a[:], ACT.Abs_reciprocal_sqrt)
+                nc.scalar.activation(r[:], a2[:], ACT.Square)
+
+        def cube(w):
+            q = work.tile([P, HALF], F32, name="pw_q")
+            nc.scalar.activation(q[:], w[:], ACT.Square, scale=math.sqrt(0.216))
+            c = work.tile([P, HALF], F32, name="pw_c")
+            nc.vector.tensor_tensor(c[:], q[:], w[:], ALU.mult)
+            back = ps_b.tile([P, HALF], F32, name="back")
+            for b in range(BLOCKS):
+                nc.tensor.transpose(blk(back, b), blk(c, b), ident[:])
+            return back
+
+        def store(t, h, back, o):
+            cols = slice(h * HALF, (h + 1) * HALF)
+            nc.vector.tensor_tensor(o[:], back[:], rated_sb[:, cols], ALU.min)
+            nc.sync.dma_start(out[t * P : (t + 1) * P, cols], o[:])
+
+        for t, h in units:
+            thrust(0, t, h, nsp[t, h], -0.3)
+
+        steps = [(ps, t, h) for ps in range(2) for t, h in units]
+        last = len(steps) - 1
+        roots, waked, spent, terms, sums, cubes = {}, {}, {}, {}, {}, {}
+        for i in range(last + 3):
+            if i <= last:
+                terms[i] = [
+                    roots[i - 2] if i - 2 in roots else fresh("term0_%d" % i),
+                    fresh("term1_%d" % i),
+                    spent[i - 2] if i - 2 in spent else fresh("term2_%d" % i),
+                ]
+                sums[i] = gathers(*steps[i], terms[i])
+            if i - 2 in cubes:
+                store(*steps[i - 2][1:], cubes[i - 2], terms[i][0] if i in terms else fresh("out%d" % i))
+            k = i - 1
+            if 0 <= k <= last:
+                ps, t, h = steps[k]
+                roots[k] = fresh("root%d" % k)
+                a = waked[k - 1] if k - 1 in spent else fresh("rs%d" % k)
+                root(sums[k], a, roots[k], k == last)
+                waked[k] = fresh("waked%d" % k)
+                nc.vector.scalar_tensor_tensor(waked[k][:], roots[k][:], 1.0, nsp[t, h][:], ALU.subtract, ALU.mult)
+                if ps == 0:
+                    spent[k] = thrust(1, t, h, waked[k], 0.3)
+                else:
+                    cubes[k] = cube(waked[k])

@@ -2,7 +2,6 @@ import math
 from contextlib import ExitStack
 
 import concourse.mybir as mybir
-from concourse.masks import make_identity
 
 F32 = mybir.dt.float32
 BF16 = mybir.dt.bfloat16
@@ -13,190 +12,367 @@ U8 = mybir.dt.uint8
 FP8X4 = mybir.dt.float8_e4m3fn_x4
 ALU = mybir.AluOpType
 ACT = mybir.ActivationFunctionType
+RSQ = ACT.Abs_reciprocal_sqrt
 
 K, T, S, N, D = 512, 2048, 512, 256, 3
+FLOPS = 2 * K * N * S
+
 P = 128
 PACK = 4
 TILES = N // P
-HALVES = 2
-HALF = S // HALVES
-BLOCKS = HALF // P
-FLOPS = 2 * K * N * S
+BLOCKS = S // P
+HALF = S // 2
+PER_COLUMN = 16
 
 SHIFT = 5.0 / 6.0
-TINY = 2.0 ** -60
+LN_FLOOR = 2.0**-60
+THR_FLOOR = 2.0**-40
 EPS = 0.0004
+CUBE = 0.6**3
+
+WIDE, MID, LAST = (0, 256), (256, 128), (384, 128)
+PIECES = (WIDE, MID, LAST)
+POOL_WORDS = 320
+RING = 20
 
 
 def tile_picked_ywakef_two_p_kernel(tc, x_words, x_scales, w1, geo, thr, rated, offs, pos1, pos2, pos3, out):
     nc = tc.nc
     with ExitStack() as ctx:
         keep = ctx.enter_context(tc.tile_pool(name="keep", bufs=1))
-        work = ctx.enter_context(tc.tile_pool(name="work", bufs=2))
-        ps_y = ctx.enter_context(tc.psum_pool(name="ps_y", bufs=1))
-        ps_s = ctx.enter_context(tc.psum_pool(name="ps_s", bufs=3))
-        ps_b = ctx.enter_context(tc.psum_pool(name="ps_b", bufs=3))
+        rings = ctx.enter_context(tc.tile_pool(name="rings", bufs=RING))
+        banks = ctx.enter_context(tc.psum_pool(name="banks", bufs=7))
+        held = ctx.enter_context(tc.psum_pool(name="held", bufs=1))
 
-        offs_sb = keep.tile([P, S // 16], U16, name="offs_sb")
-        pos_sb = [keep.tile([P, S // 16], U16, name="pos_sb%d" % d) for d in range(D)]
-        words = keep.tile([P, T], I32, name="words", align_bytes=64)
-        scales = keep.tile([P, T], U8, name="scales", align_bytes=64)
-        w_raw = keep.tile([P, PACK, N], F32, name="w_raw")
-        geo_sb = keep.tile([P, D, S], F32, name="geo_sb")
-        geo2 = keep.tile([P, D, S], F32, name="geo2")
-        thr_t = keep.tile([P, S // P], F32, name="thr_t")
-        rated_sb = keep.tile([P, S], F32, name="rated_sb")
-        quarter = keep.tile([P, S // P], F32, name="quarter")
-        warm = keep.tile([P, 1], F32, name="warm")
-        ident = keep.tile([P, P], F32, name="ident")
-
-        nc.vector.memset(scales[:].bitcast(I32), 0)
-        nc.gpsimd.memset(quarter[:], 0.25)
-        nc.scalar.activation(warm[:], quarter[:, 0:1], ACT.Sigmoid)
-        make_identity(nc, ident[:])
-
-        nc.sync.dma_start(offs_sb[:], offs)
-        nc.sync.dma_start(w_raw[:], w1.rearrange("(p j) n -> p j n", j=PACK))
-        for q in range(4):
-            nc.sync.dma_start(scales[32 * q : 32 * q + 4, :].bitcast(I32), x_scales[0, 4 * q : 4 * q + 4, :].bitcast(I32))
-        nc.sync.dma_start(words[:], x_words[0].rearrange("p n t -> p (n t)").bitcast(I32))
-        nc.sync.dma_start(geo_sb[:], geo.rearrange("d p s -> p d s"))
-        with nc.allow_non_contiguous_dma(reason="one thrust factor a partition"):
-            nc.sync.dma_start(thr_t[:], thr[0, :].rearrange("(b p) -> p b", p=P))
-        for dst, src in zip(pos_sb, (pos1, pos2, pos3)):
-            nc.sync.dma_start(dst[:], src)
-        nc.sync.dma_start(rated_sb[:], rated)
-
-        w_bf = keep.tile([P, N, PACK], BF16, name="w_bf", align_bytes=64)
-        nc.scalar.activation(w_bf[:], w_raw[:].rearrange("p j n -> p n j"), ACT.Copy, scale=-1.0)
-        xs = keep.tile([P, S], U8, name="xs", align_bytes=64)
-        nc.vector.tensor_copy(xs[:], scales[:].indirect(offs_sb[:]))
-        w_codes = keep.tile([P, N], U32, name="w_codes", align_bytes=64)
-        w_scales = keep.tile([P, N], U8, name="w_scales", align_bytes=64)
-        nc.vector.quantize_mx(out=w_codes[:].bitcast(FP8X4), scales=w_scales[:], in_=w_bf[:].rearrange("p n j -> p (n j)"))
-
-        sig = keep.tile([P, S // P, N], F32, name="sig")
-        neg_y = []
-        for h in range(HALVES):
-            xw = keep.tile([P, HALF], U32, name="xw%d" % h, align_bytes=64)
-            nc.vector.tensor_copy(xw[:], words[:].bitcast(U32).indirect(offs_sb[:, 16 * h : 16 * (h + 1)]))
-            bank = ps_y.tile([P, BLOCKS, N], F32, name="neg_y%d" % h)
-            for b in range(BLOCKS):
-                j0 = h * HALF + b * P
-                nc.tensor.matmul_mx(
-                    out=bank[:, b, :],
-                    lhsT=xw[:, b * P : (b + 1) * P].bitcast(FP8X4),
-                    lhsT_scale=xs[:, j0 : j0 + P],
-                    rhs=w_codes[:].bitcast(FP8X4),
-                    rhs_scale=w_scales[:],
-                    start=True,
-                    stop=True,
-                )
-            nc.scalar.activation(sig[:, h * BLOCKS : (h + 1) * BLOCKS, :], bank[:], ACT.Sigmoid)
-            neg_y.append(bank)
-
-        nc.vector.tensor_tensor(geo2[:], geo_sb[:], geo_sb[:], ALU.mult)
-        thr2 = keep.tile([P, S // P], F32, name="thr2")
-        root_thr = keep.tile([P, S // P], F32, name="root_thr")
-        nc.gpsimd.tensor_tensor(thr2[:], thr_t[:], thr_t[:], ALU.mult)
-        nc.gpsimd.tensor_tensor(root_thr[:], thr2[:], quarter[:], ALU.pow)
-
-        lg = keep.tile([P, S // P, N], F32, name="lg")
-        nc.scalar.activation(lg[:], sig[:], ACT.Ln, bias=TINY, scale=math.e ** (-SHIFT))
-
-        units = [(t, h) for t in range(TILES) for h in range(HALVES)]
-        nsp = {}
-        for t, h in units:
-            nsp[t, h] = keep.tile([P, HALF], F32, name="nsp%d%d" % (t, h))
-            cols = slice(t * P, (t + 1) * P)
-            nc.vector.scalar_tensor_tensor(
-                nsp[t, h][:].rearrange("p (b m) -> p b m", b=BLOCKS), neg_y[h][:, :, cols], SHIFT, lg[:, h * BLOCKS : (h + 1) * BLOCKS, cols], ALU.subtract, ALU.min
-            )
-
-        win = {}
-        for ps in range(2):
-            for t in range(TILES):
-                win[ps, t] = keep.tile([P, S], F32, name="win%d%d" % (ps, t))
-
-        def fresh(name):
-            return keep.tile([P, HALF], F32, name=name)
+        def bank(name):
+            return banks.tile([P, S], F32, name=name, tag="tensor")
 
         def blk(x, b):
             return x[:, b * P : (b + 1) * P]
 
-        def thrust(ps, t, h, src, scale):
-            a = fresh("th_a%d%d%d" % (ps, t, h))
-            nc.scalar.activation(a[:], src[:], ACT.Abs_reciprocal_sqrt, bias=0.6, scale=scale)
-            ct = work.tile([P, HALF], F32, name="th_ct")
-            back = ps_b.tile([P, HALF], F32, name="back")
-            for b in range(BLOCKS):
-                jb = h * BLOCKS + b
-                nc.scalar.activation(blk(ct, b), blk(a, b), ACT.Square, scale=root_thr[:, jb : jb + 1])
-            for b in range(BLOCKS):
-                nc.tensor.transpose(blk(back, b), blk(ct, b), ident[:])
-            nc.scalar.activation(win[ps, t][:, h * HALF : (h + 1) * HALF], back[:], ACT.Square)
-            return a
+        def staged(shape, dtype, name):
+            return keep.tile(shape, dtype, name=name, tag="staged", bufs=7, align_bytes=64)
 
-        def gathers(ps, t, h, terms):
-            for d in range(D):
-                nc.vector.tensor_tensor(
-                    terms[d][:], win[ps, t][:].indirect(pos_sb[d][:, 16 * h : 16 * (h + 1)]), geo2[:, d, h * HALF : (h + 1) * HALF], ALU.mult
+        offs_sb = keep.tile([P, S // PER_COLUMN], U16, name="offs_sb")
+        w_raw = keep.tile([P, PACK, N], F32, name="w_raw")
+        scales = keep.tile([P, T], U8, name="scales", align_bytes=64)
+        zeros = keep.tile([P, P], F32, name="zeros")
+        thr_rows = keep.tile([P, P], F32, name="thr_rows")
+        ident = staged([P, P], F32, "ident")
+        words = staged([P, T], I32, "words")
+        geo_sb = staged([P, D, S], F32, "geo_sb")
+        pos_sb = [staged([P, S // PER_COLUMN], U16, "pos_sb%d" % d) for d in range(D)]
+        rated_sb = staged([P, S], F32, "rated_sb")
+
+        nc.gpsimd.memset(scales[:, : PACK * POOL_WORDS].bitcast(I32), 0)
+        nc.vector.memset(scales[:, PACK * POOL_WORDS :].bitcast(I32), 0)
+        nc.vector.memset(thr_rows[:], 0.0)
+        nc.gpsimd.memset(zeros[:], 0.0)
+        nc.gpsimd.affine_select(
+            out=ident[:], in_=zeros[:], compare_op=ALU.not_equal, fill=1.0, base=0, pattern=[[-1, P]], channel_multiplier=1
+        )
+        warm = keep.tile([P, 1], F32, name="warm")
+        nc.scalar.activation(warm[:], zeros[:, 0:1], ACT.Sigmoid)
+
+        nc.sync.dma_start(offs_sb[:], offs)
+        nc.sync.dma_start(w_raw[:], w1.rearrange("(p r) n -> p r n", r=PACK))
+        for q in range(4):
+            nc.sync.dma_start(scales[32 * q : 32 * q + 4, :].bitcast(I32), x_scales[0, 4 * q : 4 * q + 4, :].bitcast(I32))
+        nc.sync.dma_start(words[:], x_words[0].rearrange("p n r -> p (n r)").bitcast(I32))
+        nc.sync.dma_start(thr_rows[0:BLOCKS, :], thr[0, :].rearrange("(b p) -> b p", p=P))
+        nc.sync.dma_start(geo_sb[:], geo.rearrange("d p s -> p d s"))
+        for dst, src in zip(pos_sb, (pos1, pos2, pos3)):
+            nc.sync.dma_start(dst[:], src)
+        nc.sync.dma_start(rated_sb[:], rated)
+
+        def mx_operand(width, dtype, name):
+            return keep.tile([P, width], dtype, name=name, tag="mx", bufs=4, align_bytes=64)
+
+        w_bf = keep.tile([P, N, PACK], BF16, name="w_bf", align_bytes=64)
+        nc.scalar.activation(w_bf[:], w_raw[:].rearrange("p r n -> p n r"), ACT.Copy, scale=-1.0)
+        x_sc = mx_operand(S, U8, "x_sc")
+        nc.vector.tensor_copy(x_sc[:], scales[:].indirect(offs_sb[:]))
+        w_codes = mx_operand(N, U32, "w_codes")
+        w_sc = keep.tile([P, N], U8, name="w_sc", align_bytes=64)
+        nc.vector.quantize_mx(out=w_codes[:].bitcast(FP8X4), scales=w_sc[:], in_=w_bf[:].rearrange("p n r -> p (n r)"))
+
+        def soft_tile(width, name):
+            return keep.tile([P, 2, width], F32, name=name, tag="soft", bufs=2 + 2 * TILES)
+
+        thr_turned = bank("thr_turned")
+        nc.tensor.transpose(blk(thr_turned, 0), thr_rows[:], ident[:])
+        neg_y, sig = [], []
+        for h in range(2):
+            x_w = mx_operand(HALF, U32, "x_w%d" % h)
+            entries = offs_sb[:, h * HALF // PER_COLUMN : (h + 1) * HALF // PER_COLUMN]
+            nc.vector.tensor_copy(x_w[:], words[:].bitcast(U32).indirect(entries))
+            sig.append(soft_tile(N, "sig%d" % h))
+            for b in range(2):
+                neg_y.append(bank("neg_y%d%d" % (h, b)))
+                nc.tensor.matmul_mx(
+                    out=neg_y[-1][:, :N],
+                    lhsT=blk(x_w, b).bitcast(FP8X4),
+                    lhsT_scale=blk(x_sc, 2 * h + b),
+                    rhs=w_codes[:].bitcast(FP8X4),
+                    rhs_scale=w_sc[:],
+                    start=True,
+                    stop=True,
                 )
-            s = ps_s.tile([P, HALF], F32, name="ssum")
-            for b in range(BLOCKS):
-                for d in range(D):
-                    nc.tensor.matmul(blk(s, b), blk(terms[d], b), ident[:], is_transpose=True, start=(d == 0), stop=(d == D - 1))
-            return s
+                nc.scalar.activation(sig[h][:, b, :], neg_y[-1][:, :N], ACT.Sigmoid)
 
-        def root(s, a, r, on_vector):
-            nc.scalar.activation(a[:], s[:], ACT.Abs_reciprocal_sqrt, bias=EPS)
-            if on_vector:
-                nc.vector.scalar_tensor_tensor(r[:], s[:], EPS, a[:], ALU.add, ALU.mult)
-            else:
-                a2 = work.tile([P, HALF], F32, name="wk_a2")
-                nc.scalar.activation(a2[:], a[:], ACT.Abs_reciprocal_sqrt)
-                nc.scalar.activation(r[:], a2[:], ACT.Square)
+        def per_turbine(name):
+            return keep.tile([P, BLOCKS], F32, name=name)
 
-        def cube(w):
-            q = work.tile([P, HALF], F32, name="pw_q")
-            nc.scalar.activation(q[:], w[:], ACT.Square, scale=math.sqrt(0.216))
-            c = work.tile([P, HALF], F32, name="pw_c")
-            nc.vector.tensor_tensor(c[:], q[:], w[:], ALU.mult)
-            back = ps_b.tile([P, HALF], F32, name="back")
-            for b in range(BLOCKS):
-                nc.tensor.transpose(blk(back, b), blk(c, b), ident[:])
-            return back
+        neg_thr, abs_thr, inv_thr, slope, neg_slope, offset, rated_t, neg_rated = [
+            per_turbine(name) for name in ("neg_thr", "abs_thr", "inv_thr", "slope", "neg_slope", "offset", "rated_t", "neg_rated")
+        ]
+        nc.vector.tensor_scalar(neg_thr[:], thr_turned[:, :BLOCKS], -1.0, THR_FLOOR, ALU.mult, ALU.max)
+        nc.vector.tensor_tensor(abs_thr[:], thr_turned[:, :BLOCKS], neg_thr[:], ALU.max)
+        nc.vector.reciprocal(inv_thr[:], abs_thr[:])
+        nc.vector.tensor_scalar(slope[:], inv_thr[:], 0.3, None, ALU.mult)
+        nc.vector.tensor_scalar(neg_slope[:], inv_thr[:], -0.3, None, ALU.mult)
+        nc.vector.tensor_scalar(offset[:], inv_thr[:], 0.6, None, ALU.mult)
+        rated_turned = bank("rated_turned")
+        for b in range(BLOCKS):
+            nc.tensor.transpose(blk(rated_turned, b), blk(rated_sb, b), ident[:])
+        nc.vector.tensor_copy(rated_t[:], rated_turned[:, ::P])
+        nc.vector.tensor_scalar(neg_rated[:], rated_turned[:, ::P], -1.0, None, ALU.mult)
 
-        def store(t, h, back, o):
+        logs = {}
+        for t in range(TILES):
+            for h in range(2):
+                logs[t, h] = soft_tile(P, "log%d%d" % (t, h))
+                nc.scalar.activation(logs[t, h][:], sig[h][:, :, t * P : (t + 1) * P], ACT.Ln, bias=LN_FLOOR, scale=math.e**-SHIFT)
+
+        inv_ct = keep.tile([P, S], F32, name="inv_ct")
+        inv_ct_sq = [keep.tile([P, HALF], F32, name="inv_ct_sq%d" % h, tag="head", bufs=3) for h in range(2)]
+        neg = [keep.tile([P, S], F32, name="neg0"), keep.tile([P, S], F32, name="neg1", tag="head", bufs=3)]
+        window = [keep.tile([P, S], F32, name="window%d" % phase) for phase in range(2 * TILES)]
+
+        def neg_block(t, b):
+            nc.vector.scalar_tensor_tensor(blk(neg[t], b), blk(neg_y[b], t), SHIFT, logs[t, b // 2][:, b % 2, :], ALU.subtract, ALU.min)
+
+        made = {}
+
+        def on(engine, what, phase, piece):
+            name = "%s%d_%d" % (what, phase + 1, piece[0])
+            made[what, phase, piece] = rings.tile([P, HALF], F32, name=name, tag=engine)[:, : piece[1]]
+            return made[what, phase, piece]
+
+        turned = []
+        for h in range(2):
             cols = slice(h * HALF, (h + 1) * HALF)
-            nc.vector.tensor_tensor(o[:], back[:], rated_sb[:, cols], ALU.min)
-            nc.sync.dma_start(out[t * P : (t + 1) * P, cols], o[:])
+            for b in (2 * h, 2 * h + 1):
+                neg_block(0, b)
+            for b in (2 * h, 2 * h + 1):
+                nc.vector.tensor_scalar(blk(inv_ct, b), blk(neg[0], b), neg_slope[:, b : b + 1], offset[:, b : b + 1], ALU.mult, ALU.add)
+            nc.vector.tensor_tensor(inv_ct_sq[h][:], inv_ct[:, cols], inv_ct[:, cols], ALU.mult)
+            turned.append(bank("first%d" % h))
+            for b in range(2):
+                nc.tensor.transpose(blk(turned[h], b), blk(inv_ct_sq[h], b), ident[:])
+        for h in range(2):
+            abs_ct = on("scalar", "abs_ct", -1, (h * HALF, HALF))
+            nc.scalar.activation(abs_ct, turned[h][:, :HALF], RSQ)
+            nc.vector.tensor_tensor(window[0][:, h * HALF : (h + 1) * HALF], abs_ct, abs_ct, ALU.mult)
+        for b in range(BLOCKS):
+            neg_block(1, b)
+        geo_sq = keep.tile([P, D, S], F32, name="geo_sq")
+        for d in range(D):
+            nc.vector.tensor_tensor(geo_sq[:, d, :], geo_sb[:, d, :], geo_sb[:, d, :], ALU.mult)
 
-        for t, h in units:
-            thrust(0, t, h, nsp[t, h], -0.3)
+        def span(piece):
+            return slice(piece[0], piece[0] + piece[1])
 
-        steps = [(ps, t, h) for ps in range(2) for t, h in units]
-        last = len(steps) - 1
-        roots, waked, spent, terms, sums, cubes = {}, {}, {}, {}, {}, {}
-        for i in range(last + 3):
-            if i <= last:
-                terms[i] = [
-                    roots[i - 2] if i - 2 in roots else fresh("term0_%d" % i),
-                    fresh("term1_%d" % i),
-                    spent[i - 2] if i - 2 in spent else fresh("term2_%d" % i),
-                ]
-                sums[i] = gathers(*steps[i], terms[i])
-            if i - 2 in cubes:
-                store(*steps[i - 2][1:], cubes[i - 2], terms[i][0] if i in terms else fresh("out%d" % i))
-            k = i - 1
-            if 0 <= k <= last:
-                ps, t, h = steps[k]
-                roots[k] = fresh("root%d" % k)
-                a = waked[k - 1] if k - 1 in spent else fresh("rs%d" % k)
-                root(sums[k], a, roots[k], k == last)
-                waked[k] = fresh("waked%d" % k)
-                nc.vector.scalar_tensor_tensor(waked[k][:], roots[k][:], 1.0, nsp[t, h][:], ALU.subtract, ALU.mult)
-                if ps == 0:
-                    spent[k] = thrust(1, t, h, waked[k], 0.3)
-                else:
-                    cubes[k] = cube(waked[k])
+        def blocks(piece):
+            return list(enumerate(range(piece[0] // P, (piece[0] + piece[1]) // P)))
+
+        def gather(phase, piece, lists=range(D)):
+            entries = slice(piece[0] // PER_COLUMN, (piece[0] + piece[1]) // PER_COLUMN)
+            for d in lists:
+                looked_up = window[phase][:].indirect(pos_sb[d][:, entries])
+                nc.vector.tensor_tensor(on("vector", "term%d" % d, phase, piece), looked_up, geo_sq[:, d, span(piece)], ALU.mult)
+
+        def turn(what, phase, piece, sources):
+            made[what, phase, piece] = bank("%s%d_%d" % (what, phase + 1, piece[0]))[:, : piece[1]]
+            for i, b in blocks(piece):
+                for n, source in enumerate(sources):
+                    nc.tensor.matmul(
+                        blk(made[what, phase, piece], i), source(i, b), ident[:], is_transpose=True, start=(n == 0), stop=(n == len(sources) - 1)
+                    )
+
+        def block_of(what, phase, piece):
+            return lambda i, b: blk(made[what, phase, piece], i)
+
+        def add_terms(phase, piece):
+            turn("sum", phase, piece, [block_of("term%d" % d, phase, piece) for d in range(D)])
+
+        def inv_root(phase, piece):
+            nc.scalar.activation(on("scalar", "inv_root", phase, piece), made["sum", phase, piece], RSQ, bias=EPS)
+
+        def fourth_root(phase, piece):
+            nc.scalar.activation(on("scalar", "fourth", phase, piece), made["inv_root", phase, piece], RSQ)
+
+        def root_on_scalar(phase, piece):
+            nc.scalar.activation(on("scalar", "root", phase, piece), made["fourth", phase, piece], ACT.Square)
+
+        def root_on_vector(phase, piece):
+            root = on("vector", "root", phase, piece)
+            nc.vector.scalar_tensor_tensor(root, made["sum", phase, piece], EPS, made["inv_root", phase, piece], ALU.add, ALU.mult)
+
+        def wind(phase, piece):
+            w = on("vector", "wind", phase, piece)
+            nc.vector.scalar_tensor_tensor(w, made["root", phase, piece], 1.0, neg[phase % TILES][:, span(piece)], ALU.subtract, ALU.mult)
+
+        def root_ct(phase, piece, source, factor):
+            dst = on("scalar", "root_ct", phase, piece)
+            for i, b in blocks(piece):
+                nc.scalar.activation(blk(dst, i), blk(source, i), RSQ, bias=offset[:, b : b + 1], scale=factor[:, b : b + 1])
+
+        def waked_root_ct(phase, piece):
+            root_ct(phase, piece, made["wind", phase, piece], slope)
+
+        def ct(phase, piece):
+            nc.scalar.activation(on("scalar", "ct", phase, piece), made["root_ct", phase, piece], ACT.Square)
+
+        def turn_ct(phase, piece):
+            turn("ct_plain", phase, piece, [block_of("ct", phase, piece)])
+
+        def fill_window(phase, piece):
+            nc.scalar.activation(window[phase + TILES][:, span(piece)], made["ct_plain", phase, piece], ACT.Square)
+
+        def square(phase, piece):
+            nc.scalar.activation(on("scalar", "square", phase, piece), made["wind", phase, piece], ACT.Square, scale=math.sqrt(CUBE))
+
+        def cube(phase, piece):
+            nc.vector.tensor_tensor(on("vector", "cube", phase, piece), made["square", phase, piece], made["wind", phase, piece], ALU.mult)
+
+        def store(phase, piece):
+            t = phase % TILES
+            nc.sync.dma_start(out[t * P : (t + 1) * P, span(piece)], made["power", phase, piece])
+
+        def headroom(phase, piece):
+            dst = on("scalar", "headroom", phase, piece)
+            for i, b in blocks(piece):
+                nc.scalar.activation(blk(dst, i), blk(made["cube", phase, piece], i), ACT.Relu, bias=rated_t[:, b : b + 1], scale=-1.0)
+
+        def turn_headroom(phase, piece):
+            minus_rated = lambda i, b: neg_rated[:, b : b + 1].to_broadcast([P, P])
+            turn("neg_power", phase, piece, [block_of("headroom", phase, piece), minus_rated])
+
+        def power_on_scalar(phase, piece):
+            nc.scalar.activation(on("scalar", "power", phase, piece), made["neg_power", phase, piece], ACT.Copy, scale=-1.0)
+            store(phase, piece)
+
+        def turn_cube(phase, piece):
+            turn("cube_plain", phase, piece, [block_of("cube", phase, piece)])
+
+        def power_on_vector(phase, piece):
+            dst = on("vector", "power", phase, piece)
+            nc.vector.tensor_tensor(dst, made["cube_plain", phase, piece], rated_sb[:, span(piece)], ALU.min)
+            store(phase, piece)
+
+        def each(step, phase, pieces=PIECES):
+            for piece in pieces:
+                step(phase, piece)
+
+        def rest_of_phase(phase):
+            inv_root(phase, WIDE)
+            gather(phase, LAST)
+            add_terms(phase, LAST)
+            fourth_root(phase, WIDE)
+            inv_root(phase, MID)
+            root_on_scalar(phase, WIDE)
+            fourth_root(phase, MID)
+
+        halves = ((0, HALF), (HALF, HALF))
+        for half in halves:
+            root_ct(-1, half, neg[1][:, span(half)], neg_slope)
+        each(ct, -1, halves)
+        gather(0, WIDE, [0])
+        each(turn_ct, -1, halves)
+        gather(0, WIDE, [1, 2])
+        each(fill_window, -1, halves)
+        add_terms(0, WIDE)
+        neg_plain = held.tile([P, P], F32, name="neg_plain")
+        nc.tensor.transpose(neg_plain[:], blk(neg[1], BLOCKS - 1), ident[:])
+        neg_sq = keep.tile([P, P], F32, name="neg_sq")
+        nc.scalar.activation(neg_sq[:], neg_plain[:], ACT.Square, scale=math.sqrt(CUBE))
+        gather(0, MID)
+        add_terms(0, MID)
+        rest_of_phase(0)
+
+        for phase in (1, 2):
+            before = phase - 1
+            gather(phase, WIDE, [0])
+            inv_root(before, LAST)
+            root_on_scalar(before, MID)
+            gather(phase, WIDE, [1])
+            each(wind, before, (WIDE, MID))
+            root_on_vector(before, LAST)
+            gather(phase, WIDE, [2])
+            add_terms(phase, WIDE)
+            wind(before, LAST)
+            each(waked_root_ct, before, (WIDE, MID))
+            each(ct, before, (WIDE, MID))
+            waked_root_ct(before, LAST)
+            ct(before, LAST)
+            each(turn_ct, before)
+            gather(phase, MID)
+            add_terms(phase, MID)
+            each(fill_window, before)
+            rest_of_phase(phase)
+
+        neg_cube = on("vector", "neg_cube", 3, LAST)
+        nc.vector.tensor_tensor(neg_cube, neg_plain[:], neg_sq[:], ALU.mult)
+        gather(3, WIDE, [0])
+        inv_root(2, LAST)
+        root_on_scalar(2, MID)
+        fourth_root(2, LAST)
+        gather(3, WIDE, [1])
+        root_on_scalar(2, LAST)
+        wind(2, WIDE)
+        gather(3, WIDE, [2])
+        add_terms(3, WIDE)
+        each(wind, 2, (MID, LAST))
+        each(square, 2)
+        gather(3, MID, [0])
+        each(cube, 2)
+        inv_root(3, WIDE)
+        gather(3, MID, [1])
+        root_on_vector(3, WIDE)
+        gather(3, MID, [2])
+        add_terms(3, MID)
+        each(headroom, 2)
+        wind(3, WIDE)
+        gather(3, LAST, [0, 1])
+        square(3, WIDE)
+        inv_root(3, MID)
+        each(turn_headroom, 2)
+        root_on_vector(3, MID)
+        two = on("vector", "two_terms", 3, LAST)
+        nc.vector.tensor_tensor(two, made["term0", 3, LAST], made["term1", 3, LAST], ALU.add)
+        gather(3, LAST, [2])
+        wind(3, MID)
+        total = on("vector", "sum", 3, LAST)
+        nc.vector.scalar_tensor_tensor(total, made["term2", 3, LAST], EPS, two, ALU.add, ALU.add)
+        cube(3, WIDE)
+        square(3, MID)
+        inv = on("scalar", "inv_root", 3, LAST)
+        nc.scalar.activation(inv, total, RSQ)
+        turn_cube(3, WIDE)
+        power_on_scalar(2, WIDE)
+        power_on_scalar(2, MID)
+        power_on_scalar(2, LAST)
+        cube(3, MID)
+        root = on("vector", "root", 3, LAST)
+        nc.vector.tensor_tensor(root, total, inv, ALU.mult)
+        turn_cube(3, MID)
+        gap_sq = on("scalar", "gap_sq", 3, LAST)
+        nc.scalar.activation(gap_sq, root, ACT.Square, bias=-1.0)
+        scaled = on("vector", "scaled", 3, LAST)
+        nc.vector.scalar_tensor_tensor(scaled, root, 1.0, neg_cube, ALU.subtract, ALU.mult)
+        power_on_vector(3, WIDE)
+        made["cube_plain", 3, LAST] = on("vector", "cube", 3, LAST)
+        nc.vector.tensor_tensor(made["cube_plain", 3, LAST], gap_sq, scaled, ALU.mult)
+        power_on_vector(3, MID)
+        power_on_vector(3, LAST)

@@ -71,8 +71,6 @@ def tile_picked_ywakef_two_p_kernel(tc, x_words, x_scales, w1, geo, thr, rated, 
         nc.gpsimd.affine_select(
             out=ident[:], in_=zeros[:], compare_op=ALU.not_equal, fill=1.0, base=0, pattern=[[-1, P]], channel_multiplier=1
         )
-        warm = keep.tile([P, 1], F32, name="warm")
-        nc.scalar.activation(warm[:], zeros[:, 0:1], ACT.Sigmoid)
 
         nc.sync.dma_start(offs_sb[:], offs)
         nc.sync.dma_start(w_raw[:], w1.rearrange("(p r) n -> p r n", r=PACK))
@@ -89,24 +87,21 @@ def tile_picked_ywakef_two_p_kernel(tc, x_words, x_scales, w1, geo, thr, rated, 
             return keep.tile([P, width], dtype, name=name, tag="mx", bufs=4, align_bytes=64)
 
         w_bf = keep.tile([P, N, PACK], BF16, name="w_bf", align_bytes=64)
-        nc.scalar.activation(w_bf[:], w_raw[:].rearrange("p r n -> p n r"), ACT.Copy, scale=-1.0)
+        nc.vector.tensor_scalar(w_bf[:], w_raw[:].rearrange("p r n -> p n r"), -1.0, None, ALU.mult)
         x_sc = mx_operand(S, U8, "x_sc")
         nc.vector.tensor_copy(x_sc[:], scales[:].indirect(offs_sb[:]))
         w_codes = mx_operand(N, U32, "w_codes")
         w_sc = keep.tile([P, N], U8, name="w_sc", align_bytes=64)
         nc.vector.quantize_mx(out=w_codes[:].bitcast(FP8X4), scales=w_sc[:], in_=w_bf[:].rearrange("p n r -> p (n r)"))
 
-        def soft_tile(width, name):
-            return keep.tile([P, 2, width], F32, name=name, tag="soft", bufs=2 + 2 * TILES)
-
         thr_turned = bank("thr_turned")
         nc.tensor.transpose(blk(thr_turned, 0), thr_rows[:], ident[:])
-        neg_y, sig = [], []
+        sig = keep.tile([P, BLOCKS, N], F32, name="sig")
+        neg_y = []
         for h in range(2):
             x_w = mx_operand(HALF, U32, "x_w%d" % h)
             entries = offs_sb[:, h * HALF // PER_COLUMN : (h + 1) * HALF // PER_COLUMN]
             nc.vector.tensor_copy(x_w[:], words[:].bitcast(U32).indirect(entries))
-            sig.append(soft_tile(N, "sig%d" % h))
             for b in range(2):
                 neg_y.append(bank("neg_y%d%d" % (h, b)))
                 nc.tensor.matmul_mx(
@@ -118,39 +113,33 @@ def tile_picked_ywakef_two_p_kernel(tc, x_words, x_scales, w1, geo, thr, rated, 
                     start=True,
                     stop=True,
                 )
-                nc.scalar.activation(sig[h][:, b, :], neg_y[-1][:, :N], ACT.Sigmoid)
+                nc.scalar.activation(sig[:, 2 * h + b, :], neg_y[-1][:, :N], ACT.Sigmoid)
 
-        def per_turbine(name):
-            return keep.tile([P, BLOCKS], F32, name=name)
-
-        neg_thr, abs_thr, inv_thr, slope, neg_slope, offset, rated_t, neg_rated = [
-            per_turbine(name) for name in ("neg_thr", "abs_thr", "inv_thr", "slope", "neg_slope", "offset", "rated_t", "neg_rated")
+        neg_thr, abs_thr, inv_thr, slope, neg_slope, slope_sq, offset = [
+            keep.tile([P, BLOCKS], F32, name=name) for name in ("neg_thr", "abs_thr", "inv_thr", "slope", "neg_slope", "slope_sq", "offset")
         ]
         nc.vector.tensor_scalar(neg_thr[:], thr_turned[:, :BLOCKS], -1.0, THR_FLOOR, ALU.mult, ALU.max)
         nc.vector.tensor_tensor(abs_thr[:], thr_turned[:, :BLOCKS], neg_thr[:], ALU.max)
         nc.vector.reciprocal(inv_thr[:], abs_thr[:])
         nc.vector.tensor_scalar(slope[:], inv_thr[:], 0.3, None, ALU.mult)
         nc.vector.tensor_scalar(neg_slope[:], inv_thr[:], -0.3, None, ALU.mult)
+        nc.vector.tensor_tensor(slope_sq[:], slope[:], slope[:], ALU.mult)
         nc.vector.tensor_scalar(offset[:], inv_thr[:], 0.6, None, ALU.mult)
-        rated_turned = bank("rated_turned")
-        for b in range(BLOCKS):
-            nc.tensor.transpose(blk(rated_turned, b), blk(rated_sb, b), ident[:])
-        nc.vector.tensor_copy(rated_t[:], rated_turned[:, ::P])
-        nc.vector.tensor_scalar(neg_rated[:], rated_turned[:, ::P], -1.0, None, ALU.mult)
 
-        logs = {}
+        shifts = (SHIFT + 2.0, SHIFT)
+        logs = [keep.tile([P, BLOCKS, P], F32, name="log%d" % t) for t in range(TILES)]
         for t in range(TILES):
-            for h in range(2):
-                logs[t, h] = soft_tile(P, "log%d%d" % (t, h))
-                nc.scalar.activation(logs[t, h][:], sig[h][:, :, t * P : (t + 1) * P], ACT.Ln, bias=LN_FLOOR, scale=math.e**-SHIFT)
+            nc.scalar.activation(logs[t][:], sig[:, :, t * P : (t + 1) * P], ACT.Ln, bias=LN_FLOOR, scale=math.e ** -shifts[t])
 
-        inv_ct = keep.tile([P, S], F32, name="inv_ct")
-        inv_ct_sq = [keep.tile([P, HALF], F32, name="inv_ct_sq%d" % h, tag="head", bufs=3) for h in range(2)]
-        neg = [keep.tile([P, S], F32, name="neg0"), keep.tile([P, S], F32, name="neg1", tag="head", bufs=3)]
-        window = [keep.tile([P, S], F32, name="window%d" % phase) for phase in range(2 * TILES)]
+        low = keep.tile([P, S], F32, name="low")
+        inv_ct_sq = [keep.tile([P, HALF], F32, name="inv_ct_sq%d" % h, tag="head", bufs=5) for h in range(2)]
+        neg1 = keep.tile([P, S], F32, name="neg1", tag="head", bufs=5)
+        window = [keep.tile([P, S], F32, name="window0", tag="head", bufs=5)]
+        neg = [keep.tile([P, S], F32, name="neg0", tag="head", bufs=5), neg1]
+        window.extend(keep.tile([P, S], F32, name="window%d" % phase) for phase in range(1, 2 * TILES))
 
-        def neg_block(t, b):
-            nc.vector.scalar_tensor_tensor(blk(neg[t], b), blk(neg_y[b], t), SHIFT, logs[t, b // 2][:, b % 2, :], ALU.subtract, ALU.min)
+        def soft_block(dst, t, b):
+            nc.vector.scalar_tensor_tensor(blk(dst, b), blk(neg_y[b], t), shifts[t], logs[t][:, b, :], ALU.subtract, ALU.min)
 
         made = {}
 
@@ -161,12 +150,10 @@ def tile_picked_ywakef_two_p_kernel(tc, x_words, x_scales, w1, geo, thr, rated, 
 
         turned = []
         for h in range(2):
-            cols = slice(h * HALF, (h + 1) * HALF)
             for b in (2 * h, 2 * h + 1):
-                neg_block(0, b)
+                soft_block(low, 0, b)
             for b in (2 * h, 2 * h + 1):
-                nc.vector.tensor_scalar(blk(inv_ct, b), blk(neg[0], b), neg_slope[:, b : b + 1], offset[:, b : b + 1], ALU.mult, ALU.add)
-            nc.vector.tensor_tensor(inv_ct_sq[h][:], inv_ct[:, cols], inv_ct[:, cols], ALU.mult)
+                nc.vector.scalar_tensor_tensor(blk(inv_ct_sq[h], b % 2), blk(low, b), slope_sq[:, b : b + 1], blk(low, b), ALU.mult, ALU.mult)
             turned.append(bank("first%d" % h))
             for b in range(2):
                 nc.tensor.transpose(blk(turned[h], b), blk(inv_ct_sq[h], b), ident[:])
@@ -175,7 +162,7 @@ def tile_picked_ywakef_two_p_kernel(tc, x_words, x_scales, w1, geo, thr, rated, 
             nc.scalar.activation(abs_ct, turned[h][:, :HALF], RSQ)
             nc.vector.tensor_tensor(window[0][:, h * HALF : (h + 1) * HALF], abs_ct, abs_ct, ALU.mult)
         for b in range(BLOCKS):
-            neg_block(1, b)
+            soft_block(neg[1], 1, b)
         geo_sq = keep.tile([P, D, S], F32, name="geo_sq")
         for d in range(D):
             nc.vector.tensor_tensor(geo_sq[:, d, :], geo_sb[:, d, :], geo_sb[:, d, :], ALU.mult)
@@ -192,22 +179,22 @@ def tile_picked_ywakef_two_p_kernel(tc, x_words, x_scales, w1, geo, thr, rated, 
                 looked_up = window[phase][:].indirect(pos_sb[d][:, entries])
                 nc.vector.tensor_tensor(on("vector", "term%d" % d, phase, piece), looked_up, geo_sq[:, d, span(piece)], ALU.mult)
 
-        def turn(what, phase, piece, sources):
-            made[what, phase, piece] = bank("%s%d_%d" % (what, phase + 1, piece[0]))[:, : piece[1]]
+        def turn(what, phase, piece):
+            dst = made[what + "_plain", phase, piece] = bank("%s_plain%d_%d" % (what, phase + 1, piece[0]))[:, : piece[1]]
             for i, b in blocks(piece):
-                for n, source in enumerate(sources):
-                    nc.tensor.matmul(
-                        blk(made[what, phase, piece], i), source(i, b), ident[:], is_transpose=True, start=(n == 0), stop=(n == len(sources) - 1)
-                    )
-
-        def block_of(what, phase, piece):
-            return lambda i, b: blk(made[what, phase, piece], i)
+                nc.tensor.matmul(blk(dst, i), blk(made[what, phase, piece], i), ident[:], is_transpose=True, start=True, stop=True)
 
         def add_terms(phase, piece):
-            turn("sum", phase, piece, [block_of("term%d" % d, phase, piece) for d in range(D)])
+            sums = made["sum", phase, piece] = [blk(bank("sum%d_%d" % (phase + 1, b)), 0) for i, b in blocks(piece)]
+            for d in range(D):
+                for i, b in blocks(piece):
+                    term = blk(made["term%d" % d, phase, piece], i)
+                    nc.tensor.matmul(sums[i], term, ident[:], is_transpose=True, start=(d == 0), stop=(d == D - 1))
 
         def inv_root(phase, piece):
-            nc.scalar.activation(on("scalar", "inv_root", phase, piece), made["sum", phase, piece], RSQ, bias=EPS)
+            dst = on("scalar", "inv_root", phase, piece)
+            for i, b in blocks(piece):
+                nc.scalar.activation(blk(dst, i), made["sum", phase, piece][i], RSQ, bias=EPS)
 
         def fourth_root(phase, piece):
             nc.scalar.activation(on("scalar", "fourth", phase, piece), made["inv_root", phase, piece], RSQ)
@@ -217,7 +204,9 @@ def tile_picked_ywakef_two_p_kernel(tc, x_words, x_scales, w1, geo, thr, rated, 
 
         def root_on_vector(phase, piece):
             root = on("vector", "root", phase, piece)
-            nc.vector.scalar_tensor_tensor(root, made["sum", phase, piece], EPS, made["inv_root", phase, piece], ALU.add, ALU.mult)
+            for i, b in blocks(piece):
+                inv = blk(made["inv_root", phase, piece], i)
+                nc.vector.scalar_tensor_tensor(blk(root, i), made["sum", phase, piece][i], EPS, inv, ALU.add, ALU.mult)
 
         def wind(phase, piece):
             w = on("vector", "wind", phase, piece)
@@ -235,7 +224,7 @@ def tile_picked_ywakef_two_p_kernel(tc, x_words, x_scales, w1, geo, thr, rated, 
             nc.scalar.activation(on("scalar", "ct", phase, piece), made["root_ct", phase, piece], ACT.Square)
 
         def turn_ct(phase, piece):
-            turn("ct_plain", phase, piece, [block_of("ct", phase, piece)])
+            turn("ct", phase, piece)
 
         def fill_window(phase, piece):
             nc.scalar.activation(window[phase + TILES][:, span(piece)], made["ct_plain", phase, piece], ACT.Square)
@@ -246,30 +235,14 @@ def tile_picked_ywakef_two_p_kernel(tc, x_words, x_scales, w1, geo, thr, rated, 
         def cube(phase, piece):
             nc.vector.tensor_tensor(on("vector", "cube", phase, piece), made["square", phase, piece], made["wind", phase, piece], ALU.mult)
 
-        def store(phase, piece):
-            t = phase % TILES
-            nc.sync.dma_start(out[t * P : (t + 1) * P, span(piece)], made["power", phase, piece])
-
-        def headroom(phase, piece):
-            dst = on("scalar", "headroom", phase, piece)
-            for i, b in blocks(piece):
-                nc.scalar.activation(blk(dst, i), blk(made["cube", phase, piece], i), ACT.Relu, bias=rated_t[:, b : b + 1], scale=-1.0)
-
-        def turn_headroom(phase, piece):
-            minus_rated = lambda i, b: neg_rated[:, b : b + 1].to_broadcast([P, P])
-            turn("neg_power", phase, piece, [block_of("headroom", phase, piece), minus_rated])
-
-        def power_on_scalar(phase, piece):
-            nc.scalar.activation(on("scalar", "power", phase, piece), made["neg_power", phase, piece], ACT.Copy, scale=-1.0)
-            store(phase, piece)
-
         def turn_cube(phase, piece):
-            turn("cube_plain", phase, piece, [block_of("cube", phase, piece)])
+            turn("cube", phase, piece)
 
-        def power_on_vector(phase, piece):
+        def power(phase, piece):
+            t = phase % TILES
             dst = on("vector", "power", phase, piece)
             nc.vector.tensor_tensor(dst, made["cube_plain", phase, piece], rated_sb[:, span(piece)], ALU.min)
-            store(phase, piece)
+            nc.sync.dma_start(out[t * P : (t + 1) * P, span(piece)], dst)
 
         def each(step, phase, pieces=PIECES):
             for piece in pieces:
@@ -293,6 +266,7 @@ def tile_picked_ywakef_two_p_kernel(tc, x_words, x_scales, w1, geo, thr, rated, 
         gather(0, WIDE, [1, 2])
         each(fill_window, -1, halves)
         add_terms(0, WIDE)
+        nc.scalar.activation(neg[0][:], low[:], ACT.Identity, bias=2.0)
         neg_plain = held.tile([P, P], F32, name="neg_plain")
         nc.tensor.transpose(neg_plain[:], blk(neg[1], BLOCKS - 1), ident[:])
         neg_sq = keep.tile([P, P], F32, name="neg_sq")
@@ -338,41 +312,40 @@ def tile_picked_ywakef_two_p_kernel(tc, x_words, x_scales, w1, geo, thr, rated, 
         gather(3, MID, [0])
         each(cube, 2)
         inv_root(3, WIDE)
-        gather(3, MID, [1])
-        root_on_vector(3, WIDE)
-        gather(3, MID, [2])
+        gather(3, MID, [1, 2])
         add_terms(3, MID)
-        each(headroom, 2)
+        root_on_vector(3, WIDE)
+        each(turn_cube, 2)
+        gather(3, LAST, [0])
         wind(3, WIDE)
-        gather(3, LAST, [0, 1])
-        square(3, WIDE)
         inv_root(3, MID)
-        each(turn_headroom, 2)
+        gather(3, LAST, [1])
+        square(3, WIDE)
         root_on_vector(3, MID)
-        two = on("vector", "two_terms", 3, LAST)
-        nc.vector.tensor_tensor(two, made["term0", 3, LAST], made["term1", 3, LAST], ALU.add)
+
+        two_terms = on("vector", "two_terms", 3, LAST)
+        nc.vector.tensor_tensor(two_terms, made["term0", 3, LAST], made["term1", 3, LAST], ALU.add)
         gather(3, LAST, [2])
         wind(3, MID)
-        total = on("vector", "sum", 3, LAST)
-        nc.vector.scalar_tensor_tensor(total, made["term2", 3, LAST], EPS, two, ALU.add, ALU.add)
+        total = on("vector", "total", 3, LAST)
+        nc.vector.scalar_tensor_tensor(total, made["term2", 3, LAST], EPS, two_terms, ALU.add, ALU.add)
         cube(3, WIDE)
         square(3, MID)
-        inv = on("scalar", "inv_root", 3, LAST)
-        nc.scalar.activation(inv, total, RSQ)
+        inv_total_root = on("scalar", "inv_root", 3, LAST)
+        nc.scalar.activation(inv_total_root, total, RSQ)
         turn_cube(3, WIDE)
-        power_on_scalar(2, WIDE)
-        power_on_scalar(2, MID)
-        power_on_scalar(2, LAST)
+        power(2, WIDE)
         cube(3, MID)
-        root = on("vector", "root", 3, LAST)
-        nc.vector.tensor_tensor(root, total, inv, ALU.mult)
+        last_root = on("vector", "root", 3, LAST)
+        nc.vector.tensor_tensor(last_root, total, inv_total_root, ALU.mult)
         turn_cube(3, MID)
-        gap_sq = on("scalar", "gap_sq", 3, LAST)
-        nc.scalar.activation(gap_sq, root, ACT.Square, bias=-1.0)
+        deficit_sq = on("scalar", "deficit_sq", 3, LAST)
+        nc.scalar.activation(deficit_sq, last_root, ACT.Square, bias=-1.0)
+        power(2, MID)
         scaled = on("vector", "scaled", 3, LAST)
-        nc.vector.scalar_tensor_tensor(scaled, root, 1.0, neg_cube, ALU.subtract, ALU.mult)
-        power_on_vector(3, WIDE)
-        made["cube_plain", 3, LAST] = on("vector", "cube", 3, LAST)
-        nc.vector.tensor_tensor(made["cube_plain", 3, LAST], gap_sq, scaled, ALU.mult)
-        power_on_vector(3, MID)
-        power_on_vector(3, LAST)
+        nc.vector.scalar_tensor_tensor(scaled, last_root, 1.0, neg_cube, ALU.subtract, ALU.mult)
+        power(3, WIDE)
+        nc.vector.tensor_tensor(on("vector", "cube_plain", 3, LAST), deficit_sq, scaled, ALU.mult)
+        power(2, LAST)
+        power(3, MID)
+        power(3, LAST)

@@ -27,6 +27,7 @@ PER_COLUMN = 16
 SHIFT = 5.0 / 6.0
 LN_FLOOR = 2.0**-60
 THR_FLOOR = 2.0**-40
+LOW = 2.0
 EPS = 0.0004
 CUBE = 0.6**3
 
@@ -34,6 +35,7 @@ WIDE, MID, LAST = (0, 256), (256, 128), (384, 128)
 PIECES = (WIDE, MID, LAST)
 POOL_WORDS = 320
 RING = 20
+RING_BANKS = 7
 
 
 def tile_picked_ywakef_two_p_kernel(tc, x_words, x_scales, w1, geo, thr, rated, offs, pos1, pos2, pos3, out):
@@ -41,7 +43,7 @@ def tile_picked_ywakef_two_p_kernel(tc, x_words, x_scales, w1, geo, thr, rated, 
     with ExitStack() as ctx:
         keep = ctx.enter_context(tc.tile_pool(name="keep", bufs=1))
         rings = ctx.enter_context(tc.tile_pool(name="rings", bufs=RING))
-        banks = ctx.enter_context(tc.psum_pool(name="banks", bufs=7))
+        banks = ctx.enter_context(tc.psum_pool(name="banks", bufs=RING_BANKS))
         held = ctx.enter_context(tc.psum_pool(name="held", bufs=1))
 
         def bank(name):
@@ -126,7 +128,7 @@ def tile_picked_ywakef_two_p_kernel(tc, x_words, x_scales, w1, geo, thr, rated, 
         nc.vector.tensor_tensor(slope_sq[:], slope[:], slope[:], ALU.mult)
         nc.vector.tensor_scalar(offset[:], inv_thr[:], 0.6, None, ALU.mult)
 
-        shifts = (SHIFT + 2.0, SHIFT)
+        shifts = (SHIFT + LOW, SHIFT)
         logs = [keep.tile([P, BLOCKS, P], F32, name="log%d" % t) for t in range(TILES)]
         for t in range(TILES):
             nc.scalar.activation(logs[t][:], sig[:, :, t * P : (t + 1) * P], ACT.Ln, bias=LN_FLOOR, scale=math.e ** -shifts[t])
@@ -148,18 +150,18 @@ def tile_picked_ywakef_two_p_kernel(tc, x_words, x_scales, w1, geo, thr, rated, 
             made[what, phase, piece] = rings.tile([P, HALF], F32, name=name, tag=engine)[:, : piece[1]]
             return made[what, phase, piece]
 
-        turned = []
+        first = []
         for h in range(2):
             for b in (2 * h, 2 * h + 1):
                 soft_block(low, 0, b)
             for b in (2 * h, 2 * h + 1):
                 nc.vector.scalar_tensor_tensor(blk(inv_ct_sq[h], b % 2), blk(low, b), slope_sq[:, b : b + 1], blk(low, b), ALU.mult, ALU.mult)
-            turned.append(bank("first%d" % h))
+            first.append(bank("first%d" % h))
             for b in range(2):
-                nc.tensor.transpose(blk(turned[h], b), blk(inv_ct_sq[h], b), ident[:])
+                nc.tensor.transpose(blk(first[h], b), blk(inv_ct_sq[h], b), ident[:])
         for h in range(2):
-            abs_ct = on("scalar", "abs_ct", -1, (h * HALF, HALF))
-            nc.scalar.activation(abs_ct, turned[h][:, :HALF], RSQ)
+            abs_ct = on("scalar", "abs_ct", 0, (h * HALF, HALF))
+            nc.scalar.activation(abs_ct, first[h][:, :HALF], RSQ)
             nc.vector.tensor_tensor(window[0][:, h * HALF : (h + 1) * HALF], abs_ct, abs_ct, ALU.mult)
         for b in range(BLOCKS):
             soft_block(neg[1], 1, b)
@@ -266,7 +268,7 @@ def tile_picked_ywakef_two_p_kernel(tc, x_words, x_scales, w1, geo, thr, rated, 
         gather(0, WIDE, [1, 2])
         each(fill_window, -1, halves)
         add_terms(0, WIDE)
-        nc.scalar.activation(neg[0][:], low[:], ACT.Identity, bias=2.0)
+        nc.scalar.activation(neg[0][:], low[:], ACT.Identity, bias=LOW)
         neg_plain = held.tile([P, P], F32, name="neg_plain")
         nc.tensor.transpose(neg_plain[:], blk(neg[1], BLOCKS - 1), ident[:])
         neg_sq = keep.tile([P, P], F32, name="neg_sq")
@@ -281,15 +283,14 @@ def tile_picked_ywakef_two_p_kernel(tc, x_words, x_scales, w1, geo, thr, rated, 
             inv_root(before, LAST)
             root_on_scalar(before, MID)
             gather(phase, WIDE, [1])
-            each(wind, before, (WIDE, MID))
+            wind(before, WIDE)
             root_on_vector(before, LAST)
+            wind(before, MID)
+            wind(before, LAST)
             gather(phase, WIDE, [2])
             add_terms(phase, WIDE)
-            wind(before, LAST)
-            each(waked_root_ct, before, (WIDE, MID))
-            each(ct, before, (WIDE, MID))
-            waked_root_ct(before, LAST)
-            ct(before, LAST)
+            each(waked_root_ct, before)
+            each(ct, before)
             each(turn_ct, before)
             gather(phase, MID)
             add_terms(phase, MID)

import math
from contextlib import ExitStack

import concourse.mybir as mybir

F32 = mybir.dt.float32
BF16 = mybir.dt.bfloat16
I32 = mybir.dt.int32
U32 = mybir.dt.uint32
U16 = mybir.dt.uint16
U8 = mybir.dt.uint8
FP8X4 = mybir.dt.float8_e4m3fn_x4
ALU = mybir.AluOpType
ACT = mybir.ActivationFunctionType
RSQ = ACT.Abs_reciprocal_sqrt

K, T, S, N, D = 512, 2048, 512, 256, 3
FLOPS = 2 * K * N * S

P = 128
PACK = 4
TILES = N // P
BLOCKS = S // P
HALF = S // 2
PER_COLUMN = 16

SHIFT = 5.0 / 6.0
LN_FLOOR = 2.0**-60
THR_FLOOR = 2.0**-40
LOW = 2.0
EPS = 0.0004
CUBE = 0.6**3

WIDE, MID, LAST = (0, 256), (256, 128), (384, 128)
PIECES = (WIDE, MID, LAST)
POOL_WORDS = 320
RING = 20
RING_BANKS = 7


def tile_picked_ywakef_two_p_kernel(tc, x_words, x_scales, w1, geo, thr, rated, offs, pos1, pos2, pos3, out):
    nc = tc.nc
    with ExitStack() as ctx:
        keep = ctx.enter_context(tc.tile_pool(name="keep", bufs=1))
        rings = ctx.enter_context(tc.tile_pool(name="rings", bufs=RING))
        banks = ctx.enter_context(tc.psum_pool(name="banks", bufs=RING_BANKS))
        held = ctx.enter_context(tc.psum_pool(name="held", bufs=1))

        def bank(name):
            return banks.tile([P, S], F32, name=name, tag="tensor")

        def blk(x, b):
            return x[:, b * P : (b + 1) * P]

        def staged(shape, dtype, name):
            return keep.tile(shape, dtype, name=name, tag="staged", bufs=7, align_bytes=64)

        offs_sb = keep.tile([P, S // PER_COLUMN], U16, name="offs_sb")
        w_raw = keep.tile([P, PACK, N], F32, name="w_raw")
        scales = keep.tile([P, T], U8, name="scales", align_bytes=64)
        zeros = keep.tile([P, P], F32, name="zeros")
        thr_rows = keep.tile([P, P], F32, name="thr_rows")
        ident = staged([P, P], F32, "ident")
        words = staged([P, T], I32, "words")
        geo_sb = staged([P, D, S], F32, "geo_sb")
        pos_sb = [staged([P, S // PER_COLUMN], U16, "pos_sb%d" % d) for d in range(D)]
        rated_sb = staged([P, S], F32, "rated_sb")

        nc.gpsimd.memset(scales[:, : PACK * POOL_WORDS].bitcast(I32), 0)
        nc.vector.memset(scales[:, PACK * POOL_WORDS :].bitcast(I32), 0)
        nc.vector.memset(thr_rows[:], 0.0)
        nc.gpsimd.memset(zeros[:], 0.0)
        nc.gpsimd.affine_select(
            out=ident[:], in_=zeros[:], compare_op=ALU.not_equal, fill=1.0, base=0, pattern=[[-1, P]], channel_multiplier=1
        )

        nc.sync.dma_start(offs_sb[:], offs)
        nc.sync.dma_start(w_raw[:], w1.rearrange("(p r) n -> p r n", r=PACK))
        for q in range(4):
            nc.sync.dma_start(scales[32 * q : 32 * q + 4, :].bitcast(I32), x_scales[0, 4 * q : 4 * q + 4, :].bitcast(I32))
        nc.sync.dma_start(words[:], x_words[0].rearrange("p n r -> p (n r)").bitcast(I32))
        nc.sync.dma_start(thr_rows[0:BLOCKS, :], thr[0, :].rearrange("(b p) -> b p", p=P))
        nc.sync.dma_start(geo_sb[:], geo.rearrange("d p s -> p d s"))
        for dst, src in zip(pos_sb, (pos1, pos2, pos3)):
            nc.sync.dma_start(dst[:], src)
        nc.sync.dma_start(rated_sb[:], rated)

        def mx_operand(width, dtype, name):
            return keep.tile([P, width], dtype, name=name, tag="mx", bufs=4, align_bytes=64)

        w_bf = keep.tile([P, N, PACK], BF16, name="w_bf", align_bytes=64)
        nc.vector.tensor_scalar(w_bf[:], w_raw[:].rearrange("p r n -> p n r"), -1.0, None, ALU.mult)
        x_sc = mx_operand(S, U8, "x_sc")
        nc.vector.tensor_copy(x_sc[:], scales[:].indirect(offs_sb[:]))
        w_codes = mx_operand(N, U32, "w_codes")
        w_sc = keep.tile([P, N], U8, name="w_sc", align_bytes=64)
        nc.vector.quantize_mx(out=w_codes[:].bitcast(FP8X4), scales=w_sc[:], in_=w_bf[:].rearrange("p n r -> p (n r)"))

        thr_turned = bank("thr_turned")
        nc.tensor.transpose(blk(thr_turned, 0), thr_rows[:], ident[:])
        sig = keep.tile([P, BLOCKS, N], F32, name="sig")
        neg_y = []
        for h in range(2):
            x_w = mx_operand(HALF, U32, "x_w%d" % h)
            entries = offs_sb[:, h * HALF // PER_COLUMN : (h + 1) * HALF // PER_COLUMN]
            nc.vector.tensor_copy(x_w[:], words[:].bitcast(U32).indirect(entries))
            for b in range(2):
                neg_y.append(bank("neg_y%d%d" % (h, b)))
                nc.tensor.matmul_mx(
                    out=neg_y[-1][:, :N],
                    lhsT=blk(x_w, b).bitcast(FP8X4),
                    lhsT_scale=blk(x_sc, 2 * h + b),
                    rhs=w_codes[:].bitcast(FP8X4),
                    rhs_scale=w_sc[:],
                    start=True,
                    stop=True,
                )
                nc.scalar.activation(sig[:, 2 * h + b, :], neg_y[-1][:, :N], ACT.Sigmoid)

        neg_thr, abs_thr, inv_thr, slope, neg_slope, slope_sq, offset = [
            keep.tile([P, BLOCKS], F32, name=name) for name in ("neg_thr", "abs_thr", "inv_thr", "slope", "neg_slope", "slope_sq", "offset")
        ]
        nc.vector.tensor_scalar(neg_thr[:], thr_turned[:, :BLOCKS], -1.0, THR_FLOOR, ALU.mult, ALU.max)
        nc.vector.tensor_tensor(abs_thr[:], thr_turned[:, :BLOCKS], neg_thr[:], ALU.max)
        nc.vector.reciprocal(inv_thr[:], abs_thr[:])
        nc.vector.tensor_scalar(slope[:], inv_thr[:], 0.3, None, ALU.mult)
        nc.vector.tensor_scalar(neg_slope[:], inv_thr[:], -0.3, None, ALU.mult)
        nc.vector.tensor_tensor(slope_sq[:], slope[:], slope[:], ALU.mult)
        nc.vector.tensor_scalar(offset[:], inv_thr[:], 0.6, None, ALU.mult)

        shifts = (SHIFT + LOW, SHIFT)
        logs = [keep.tile([P, BLOCKS, P], F32, name="log%d" % t) for t in range(TILES)]
        for t in range(TILES):
            nc.scalar.activation(logs[t][:], sig[:, :, t * P : (t + 1) * P], ACT.Ln, bias=LN_FLOOR, scale=math.e ** -shifts[t])

        low = keep.tile([P, S], F32, name="low")
        inv_ct_sq = [keep.tile([P, HALF], F32, name="inv_ct_sq%d" % h, tag="head", bufs=5) for h in range(2)]
        neg1 = keep.tile([P, S], F32, name="neg1", tag="head", bufs=5)
        window = [keep.tile([P, S], F32, name="window0", tag="head", bufs=5)]
        neg = [keep.tile([P, S], F32, name="neg0", tag="head", bufs=5), neg1]
        window.extend(keep.tile([P, S], F32, name="window%d" % phase) for phase in range(1, 2 * TILES))

        def soft_block(dst, t, b):
            nc.vector.scalar_tensor_tensor(blk(dst, b), blk(neg_y[b], t), shifts[t], logs[t][:, b, :], ALU.subtract, ALU.min)

        made = {}

        def on(engine, what, phase, piece):
            name = "%s%d_%d" % (what, phase + 1, piece[0])
            made[what, phase, piece] = rings.tile([P, HALF], F32, name=name, tag=engine)[:, : piece[1]]
            return made[what, phase, piece]

        first = []
        for h in range(2):
            for b in (2 * h, 2 * h + 1):
                soft_block(low, 0, b)
            for b in (2 * h, 2 * h + 1):
                nc.vector.scalar_tensor_tensor(blk(inv_ct_sq[h], b % 2), blk(low, b), slope_sq[:, b : b + 1], blk(low, b), ALU.mult, ALU.mult)
            first.append(bank("first%d" % h))
            for b in range(2):
                nc.tensor.transpose(blk(first[h], b), blk(inv_ct_sq[h], b), ident[:])
        for h in range(2):
            abs_ct = on("scalar", "abs_ct", 0, (h * HALF, HALF))
            nc.scalar.activation(abs_ct, first[h][:, :HALF], RSQ)
            nc.vector.tensor_tensor(window[0][:, h * HALF : (h + 1) * HALF], abs_ct, abs_ct, ALU.mult)
        for b in range(BLOCKS):
            soft_block(neg[1], 1, b)
        geo_sq = keep.tile([P, D, S], F32, name="geo_sq")
        for d in range(D):
            nc.vector.tensor_tensor(geo_sq[:, d, :], geo_sb[:, d, :], geo_sb[:, d, :], ALU.mult)

        def span(piece):
            return slice(piece[0], piece[0] + piece[1])

        def blocks(piece):
            return list(enumerate(range(piece[0] // P, (piece[0] + piece[1]) // P)))

        def gather(phase, piece, lists=range(D)):
            entries = slice(piece[0] // PER_COLUMN, (piece[0] + piece[1]) // PER_COLUMN)
            for d in lists:
                looked_up = window[phase][:].indirect(pos_sb[d][:, entries])
                nc.vector.tensor_tensor(on("vector", "term%d" % d, phase, piece), looked_up, geo_sq[:, d, span(piece)], ALU.mult)

        def turn(what, phase, piece):
            dst = made[what + "_plain", phase, piece] = bank("%s_plain%d_%d" % (what, phase + 1, piece[0]))[:, : piece[1]]
            for i, b in blocks(piece):
                nc.tensor.matmul(blk(dst, i), blk(made[what, phase, piece], i), ident[:], is_transpose=True, start=True, stop=True)

        def add_terms(phase, piece):
            sums = made["sum", phase, piece] = [blk(bank("sum%d_%d" % (phase + 1, b)), 0) for i, b in blocks(piece)]
            for d in range(D):
                for i, b in blocks(piece):
                    term = blk(made["term%d" % d, phase, piece], i)
                    nc.tensor.matmul(sums[i], term, ident[:], is_transpose=True, start=(d == 0), stop=(d == D - 1))

        def inv_root(phase, piece):
            dst = on("scalar", "inv_root", phase, piece)
            for i, b in blocks(piece):
                nc.scalar.activation(blk(dst, i), made["sum", phase, piece][i], RSQ, bias=EPS)

        def fourth_root(phase, piece):
            nc.scalar.activation(on("scalar", "fourth", phase, piece), made["inv_root", phase, piece], RSQ)

        def root_on_scalar(phase, piece):
            nc.scalar.activation(on("scalar", "root", phase, piece), made["fourth", phase, piece], ACT.Square)

        def root_on_vector(phase, piece):
            root = on("vector", "root", phase, piece)
            for i, b in blocks(piece):
                inv = blk(made["inv_root", phase, piece], i)
                nc.vector.scalar_tensor_tensor(blk(root, i), made["sum", phase, piece][i], EPS, inv, ALU.add, ALU.mult)

        def wind(phase, piece):
            w = on("vector", "wind", phase, piece)
            nc.vector.scalar_tensor_tensor(w, made["root", phase, piece], 1.0, neg[phase % TILES][:, span(piece)], ALU.subtract, ALU.mult)

        def root_ct(phase, piece, source, factor):
            dst = on("scalar", "root_ct", phase, piece)
            for i, b in blocks(piece):
                nc.scalar.activation(blk(dst, i), blk(source, i), RSQ, bias=offset[:, b : b + 1], scale=factor[:, b : b + 1])

        def waked_root_ct(phase, piece):
            root_ct(phase, piece, made["wind", phase, piece], slope)

        def ct(phase, piece):
            nc.scalar.activation(on("scalar", "ct", phase, piece), made["root_ct", phase, piece], ACT.Square)

        def turn_ct(phase, piece):
            turn("ct", phase, piece)

        def fill_window(phase, piece):
            nc.scalar.activation(window[phase + TILES][:, span(piece)], made["ct_plain", phase, piece], ACT.Square)

        def square(phase, piece):
            nc.scalar.activation(on("scalar", "square", phase, piece), made["wind", phase, piece], ACT.Square, scale=math.sqrt(CUBE))

        def cube(phase, piece):
            nc.vector.tensor_tensor(on("vector", "cube", phase, piece), made["square", phase, piece], made["wind", phase, piece], ALU.mult)

        def turn_cube(phase, piece):
            turn("cube", phase, piece)

        def power(phase, piece):
            t = phase % TILES
            dst = on("vector", "power", phase, piece)
            nc.vector.tensor_tensor(dst, made["cube_plain", phase, piece], rated_sb[:, span(piece)], ALU.min)
            nc.sync.dma_start(out[t * P : (t + 1) * P, span(piece)], dst)

        def each(step, phase, pieces=PIECES):
            for piece in pieces:
                step(phase, piece)

        def rest_of_phase(phase):
            inv_root(phase, WIDE)
            gather(phase, LAST)
            add_terms(phase, LAST)
            fourth_root(phase, WIDE)
            inv_root(phase, MID)
            root_on_scalar(phase, WIDE)
            fourth_root(phase, MID)

        halves = ((0, HALF), (HALF, HALF))
        for half in halves:
            root_ct(-1, half, neg[1][:, span(half)], neg_slope)
        each(ct, -1, halves)
        gather(0, WIDE, [0])
        each(turn_ct, -1, halves)
        gather(0, WIDE, [1, 2])
        each(fill_window, -1, halves)
        add_terms(0, WIDE)
        nc.scalar.activation(neg[0][:], low[:], ACT.Identity, bias=LOW)
        neg_plain = held.tile([P, P], F32, name="neg_plain")
        nc.tensor.transpose(neg_plain[:], blk(neg[1], BLOCKS - 1), ident[:])
        neg_sq = keep.tile([P, P], F32, name="neg_sq")
        nc.scalar.activation(neg_sq[:], neg_plain[:], ACT.Square, scale=math.sqrt(CUBE))
        gather(0, MID)
        add_terms(0, MID)
        rest_of_phase(0)

        for phase in (1, 2):
            before = phase - 1
            gather(phase, WIDE, [0])
            inv_root(before, LAST)
            root_on_scalar(before, MID)
            gather(phase, WIDE, [1])
            wind(before, WIDE)
            root_on_vector(before, LAST)
            wind(before, MID)
            wind(before, LAST)
            gather(phase, WIDE, [2])
            add_terms(phase, WIDE)
            each(waked_root_ct, before)
            each(ct, before)
            each(turn_ct, before)
            gather(phase, MID)
            add_terms(phase, MID)
            each(fill_window, before)
            rest_of_phase(phase)

        neg_cube = on("vector", "neg_cube", 3, LAST)
        nc.vector.tensor_tensor(neg_cube, neg_plain[:], neg_sq[:], ALU.mult)
        gather(3, WIDE, [0])
        inv_root(2, LAST)
        root_on_scalar(2, MID)
        fourth_root(2, LAST)
        gather(3, WIDE, [1])
        root_on_scalar(2, LAST)
        wind(2, WIDE)
        gather(3, WIDE, [2])
        add_terms(3, WIDE)
        each(wind, 2, (MID, LAST))
        each(square, 2)
        gather(3, MID, [0])
        each(cube, 2)
        inv_root(3, WIDE)
        gather(3, MID, [1, 2])
        add_terms(3, MID)
        root_on_vector(3, WIDE)
        each(turn_cube, 2)
        gather(3, LAST, [0])
        wind(3, WIDE)
        inv_root(3, MID)
        gather(3, LAST, [1])
        square(3, WIDE)
        root_on_vector(3, MID)

        two_terms = on("vector", "two_terms", 3, LAST)
        nc.vector.tensor_tensor(two_terms, made["term0", 3, LAST], made["term1", 3, LAST], ALU.add)
        gather(3, LAST, [2])
        wind(3, MID)
        total = on("vector", "total", 3, LAST)
        nc.vector.scalar_tensor_tensor(total, made["term2", 3, LAST], EPS, two_terms, ALU.add, ALU.add)
        cube(3, WIDE)
        square(3, MID)
        inv_total_root = on("scalar", "inv_root", 3, LAST)
        nc.scalar.activation(inv_total_root, total, RSQ)
        turn_cube(3, WIDE)
        power(2, WIDE)
        cube(3, MID)
        last_root = on("vector", "root", 3, LAST)
        nc.vector.tensor_tensor(last_root, total, inv_total_root, ALU.mult)
        turn_cube(3, MID)
        deficit_sq = on("scalar", "deficit_sq", 3, LAST)
        nc.scalar.activation(deficit_sq, last_root, ACT.Square, bias=-1.0)
        power(2, MID)
        scaled = on("vector", "scaled", 3, LAST)
        nc.vector.scalar_tensor_tensor(scaled, last_root, 1.0, neg_cube, ALU.subtract, ALU.mult)
        power(3, WIDE)
        nc.vector.tensor_tensor(on("vector", "cube_plain", 3, LAST), deficit_sq, scaled, ALU.mult)
        power(2, LAST)
        power(3, MID)
        power(3, LAST)
